import numpy as np
import ml_dtypes


def mxq(x, axis, fmt="e4m3"):
    dtype, down = {"e4m3": (ml_dtypes.float8_e4m3fn, 7), "e5m2": (ml_dtypes.float8_e5m2, 14)}[fmt]
    v = np.moveaxis(np.asarray(x, np.float32).astype(ml_dtypes.bfloat16).astype(np.float64), axis, -1)
    blocks = v.reshape(v.shape[:-1] + (-1, 32))
    amax = np.abs(blocks).max(-1, keepdims=True)
    byte = np.maximum(np.where(amax > 0, np.frexp(amax)[1] - 1 + 127, 0) - down, 1)
    scale = np.exp2(byte - 127.0)
    codes = (blocks / scale).astype(np.float32).astype(dtype).astype(np.float64)
    return np.moveaxis((codes * scale).reshape(v.shape), -1, axis)


WIDE = False


def mx_kscale(k):
    if not WIDE:
        return np.ones(k)
    levels = np.array([30, -30])
    if k % 512:
        return np.exp2(np.random.permutation(np.resize(levels, k // 32))).repeat(32)
    a = np.empty((k // 512, 16))
    for p in range(k // 512):
        a[p, :8] = np.random.permutation(np.resize(levels, 8))
        for g in range(8):
            far = levels[np.abs(levels - a[p, g]) >= 10]
            a[p, g + 8] = far[np.random.randint(len(far))]
    return np.exp2(a.ravel()).repeat(32)


def f64(x):
    return np.asarray(x).astype(np.float64)


def striped(idx):
    return np.tile(np.asarray(idx).reshape(-1, 16).T, (8, 1)).astype(np.uint16)


def unstriped(offs):
    return offs[:16].T.reshape(-1).astype(np.int64)


E2M1 = np.array([0.0, 0.5, 1.0, 1.5, 2.0, 3.0, 4.0, 6.0, -0.0, -0.5, -1.0, -1.5, -2.0, -3.0, -4.0, -6.0])


def pack_weight(w, fmt):
    k, n = w.shape
    w = f64(np.asarray(w, np.float32).astype(ml_dtypes.bfloat16)).reshape(k // 32, 32, n)
    amax = np.abs(w).max(1)
    if fmt in ("e4m3", "e5m2"):
        byte = np.frexp(amax)[1] - 1 + 127 - (7 if fmt == "e4m3" else 14)
    else:
        mant, ex = np.frexp(amax / 6.0)
        byte = np.where(mant > 0.5, ex, ex - 1) + 127
    byte = np.clip(np.where(amax > 0, byte, 1), 1, 254)
    scaled = (w * np.exp2(127.0 - byte)[:, None, :]).reshape(k, n).astype(np.float32)
    by_word = np.ascontiguousarray(scaled.reshape(k // 512, 128, 4, n).transpose(0, 1, 3, 2))
    if fmt in ("e4m3", "e5m2"):
        words = by_word.astype(ml_dtypes.float8_e4m3fn if fmt == "e4m3" else ml_dtypes.float8_e5m2).view(np.uint8)
    else:
        c = by_word.astype(ml_dtypes.float4_e2m1fn).view(np.uint8) & 0xF
        words = (c[..., 0::2] | (c[..., 1::2] << 4)).reshape(k // 512, 128, 2 * n)
    return np.ascontiguousarray(words), np.ascontiguousarray(byte.astype(np.uint8).reshape(k // 512, 16, n))


def unpack_weight(words, scales, fmt):
    g, _, n = scales.shape
    words = np.ascontiguousarray(words).reshape(g, 128, n, -1)
    if fmt in ("e4m3", "e5m2"):
        vals = words.view(ml_dtypes.float8_e4m3fn if fmt == "e4m3" else ml_dtypes.float8_e5m2).astype(np.float64)
    else:
        nib = np.empty((g, 128, n, 4), np.uint8)
        nib[..., 0::2] = words & 0xF
        nib[..., 1::2] = words >> 4
        vals = E2M1[nib]
    vals = vals * np.repeat(np.exp2(scales.astype(np.float64) - 127.0), 8, axis=1)[..., None]
    return vals.transpose(0, 1, 3, 2).reshape(g * 512, n)


K, T, J, R, O, N, E = 512, 2048, 256, 512, 128, 256, 512


def setup_inputs():
    n = np.random.standard_normal
    idx = np.random.permutation(T)[:J]
    idx2 = np.random.permutation(T)[:J]
    idx3 = np.random.permutation(J)[:O]
    idx4 = np.random.permutation(J)[:O]
    idx5 = np.random.permutation(E)[:O]
    idx6 = np.random.permutation(E)[:O]
    fk = mx_kscale(K)
    fr = mx_kscale(R)
    xtp = pack_weight(n((K, T)) / fk[:, None], "e4m3")
    wp = pack_weight(n((K, R)) * 1 / np.sqrt(K) * fk[:, None] * fr, "e2m1")
    w2p = pack_weight(n((K, R)) * 1 / np.sqrt(K) * fk[:, None], "e5m2")
    wbp = pack_weight(n((R, N)) * 1 / np.sqrt(R) / fr[:, None], "e5m2")
    return {
        "xt_words": xtp[0],
        "xt_scales": xtp[1],
        "w_words": wp[0],
        "w_scales": wp[1],
        "w2_words": w2p[0],
        "w2_scales": w2p[1],
        "wb_words": wbp[0],
        "wb_scales": wbp[1],
        "offs": striped(idx),
        "offs2": striped(idx2),
        "offs3": striped(idx3),
        "offs4": striped(idx4),
        "offs5": striped(idx5),
        "offs6": striped(idx6),
    }


def reference(xt_words, xt_scales, w_words, w_scales, w2_words, w2_scales, wb_words, wb_scales, offs, offs2, offs3, offs4, offs5, offs6):
    idx = unstriped(offs)
    idx2 = unstriped(offs2)
    idx3 = unstriped(offs3)
    idx4 = unstriped(offs4)
    idx5 = unstriped(offs5)
    idx6 = unstriped(offs6)
    xtu = unpack_weight(xt_words, xt_scales, "e4m3")
    wu = unpack_weight(w_words, w_scales, "e2m1")
    w2u = unpack_weight(w2_words, w2_scales, "e5m2")
    wbu = unpack_weight(wb_words, wb_scales, "e5m2")
    xtidxg = xtu[:, idx]
    a = wu.T @ xtidxg
    xtidx2g = xtu[:, idx2]
    b = w2u.T @ xtidx2g
    lb = b[:, 0:1]
    lb2 = b[:, 128:129]
    la = a[:, 0:1]
    dl = np.abs(lb - lb2)
    hid = np.maximum(a[:, idx3] * dl, b[:, idx4] * la)
    hidq = mxq(hid, 0, "e4m3")
    p = wbu.T @ hidq
    pa = np.zeros((N, E))
    pa[:, idx5] = p
    pb = np.zeros((N, E))
    pb[:, idx6] = p
    y = pa + pb
    return y

@@ -1,0 +1,199 @@
+from contextlib import ExitStack
+
+import concourse.mybir as mybir
+
+K, T, J, R, O, N, E = 512, 2048, 256, 512, 128, 256, 512
+FLOPS = 2 * K * R * J * 2 + 2 * R * N * O
+
+F32 = mybir.dt.float32
+BF16 = mybir.dt.bfloat16
+I32 = mybir.dt.int32
+U32 = mybir.dt.uint32
+U16 = mybir.dt.uint16
+U8 = mybir.dt.uint8
+E4M3X4 = mybir.dt.float8_e4m3fn_x4
+E5M2X4 = mybir.dt.float8_e5m2_x4
+E2M1X4 = mybir.dt.float4_e2m1fn_x4
+ALU = mybir.AluOpType
+COPY = mybir.ActivationFunctionType.Copy
+
+P = 128
+PACK = 4
+QUADS = 4
+QUAD = 32
+
+
+def tile_list_contrast_ahead_one_pagetwice_kernel(
+    tc, xt_words, xt_scales, w_words, w_scales, w2_words, w2_scales, wb_words, wb_scales,
+    offs, offs2, offs3, offs4, offs5, offs6, out,
+):
+    nc = tc.nc
+    with ExitStack() as ctx:
+        sb = ctx.enter_context(tc.tile_pool(name="sb", bufs=1))
+        ps = ctx.enter_context(tc.psum_pool(name="ps", bufs=1))
+
+        def sbuf(name, shape, dtype):
+            return sb.tile(shape, dtype, name=name, align_bytes=64)
+
+        def load_list(name, src):
+            tile = sbuf(name, list(src.shape), U16)
+            nc.sync.dma_start(tile[:], src)
+            return tile
+
+        def zeroed_plane(name, columns):
+            plane = sbuf(name, [P, columns], U8)
+            nc.vector.memset(plane[:].bitcast(I32), 0)
+            return plane
+
+        def stage_rows(queue, stage, scales, half):
+            rows = scales[0, 8 * half : 8 * half + 8, :].bitcast(I32)
+            queue.dma_start(stage[64 * half : 64 * half + 4, :, :], rows.rearrange("(q r) n -> r q n", q=2))
+
+        def spread_rows(plane, stage):
+            for q in range(QUADS):
+                src = 64 * (q // 2)
+                nc.vector.tensor_copy(plane[QUAD * q : QUAD * q + 4, :].bitcast(I32), stage[src : src + 4, q % 2, :])
+
+        def load_plane(plane, scales):
+            for r in range(4):
+                nc.sync.dma_start(plane[r:P:QUAD, :].bitcast(I32), scales[0, r:16:4, :].bitcast(I32))
+
+        def load_words(queue, tile, words):
+            queue.dma_start(tile[:].bitcast(I32), words.bitcast(I32))
+
+        w2_plane = zeroed_plane("w2_plane", R)
+        x_plane = zeroed_plane("x_plane", T)
+        w_plane = zeroed_plane("w_plane", R)
+        wb_plane = zeroed_plane("wb_plane", N)
+
+        x_stage = sbuf("x_stage", [P, 2, T // 4], I32)
+        w_stage = sbuf("w_stage", [P, 2, R // 4], I32)
+        x_table = sbuf("x_table", [P, T], U32)
+        w_raw = sbuf("w_raw", [P, R], U16)
+        w2_raw = sbuf("w2_raw", [P, R], U32)
+        wb_codes = sbuf("wb_codes", [P, N], U32)
+
+        stage_rows(nc.sync, x_stage, xt_scales, 0)
+        stage_rows(nc.scalar, x_stage, xt_scales, 1)
+        list1 = load_list("list1", offs)
+        stage_rows(nc.scalar, w_stage, w_scales, 0)
+        list2 = load_list("list2", offs2)
+        stage_rows(nc.scalar, w_stage, w_scales, 1)
+        list4 = load_list("list4", offs4)
+        load_words(nc.scalar, x_table, xt_words[0].rearrange("p n t -> p (n t)"))
+        load_words(nc.scalar, w_raw, w_words[0])
+        load_words(nc.scalar, w2_raw, w2_words[0].rearrange("p n t -> p (n t)"))
+        load_plane(w2_plane, w2_scales)
+        list3 = load_list("list3", offs3)
+        load_words(nc.sync, wb_codes, wb_words[0].rearrange("p n t -> p (n t)"))
+        load_plane(wb_plane, wb_scales)
+        list5 = load_list("list5", offs5)
+        list6 = load_list("list6", offs6)
+
+        pages = {}
+        for h in range(2):
+            for name in ("pa", "pb"):
+                pages[name, h] = sbuf(f"{name}{h}", [P, E], F32)
+                nc.vector.memset(pages[name, h][:], 0.0)
+
+        spread_rows(x_plane, x_stage)
+        spread_rows(w_plane, w_stage)
+        w_dealt_plane = sbuf("w_dealt_plane", [P, PACK, P], U8)
+        w2_dealt_plane = sbuf("w2_dealt_plane", [P, PACK, P], U8)
+        nc.vector.tensor_copy(w_dealt_plane[:], w_plane[:].rearrange("p (m t) -> p t m", t=PACK))
+        nc.gpsimd.tensor_copy(w2_dealt_plane[:], w2_plane[:].rearrange("p (m t) -> p t m", t=PACK))
+
+        x1_codes = sbuf("x1_codes", [P, J], U32)
+        x2_codes = sbuf("x2_codes", [P, J], U32)
+        x1_plane = sbuf("x1_plane", [P, J], U8)
+        x2_plane = sbuf("x2_plane", [P, J], U8)
+        nc.vector.tensor_copy(x1_plane[:], x_plane[:].indirect(list1[:]))
+        nc.vector.tensor_copy(x2_plane[:], x_plane[:].indirect(list2[:]))
+        nc.vector.tensor_copy(x1_codes[:], x_table[:].indirect(list1[:]))
+        nc.vector.tensor_copy(x2_codes[:], x_table[:].indirect(list2[:]))
+
+        w_dealt = [sbuf(f"w_dealt{u}", [P, 2, P], U16) for u in range(2)]
+        w2_dealt = [sbuf(f"w2_dealt{u}", [P, 2, P], U32) for u in range(2)]
+        for u in range(2):
+            nc.scalar.copy(w_dealt[u][:], w_raw[:].rearrange("p (m t) -> p t m", t=PACK)[:, 2 * u : 2 * u + 2, :])
+        for u in range(2):
+            nc.scalar.copy(
+                w2_dealt[u][:].rearrange("p t m -> p m t"),
+                w2_raw[:].rearrange("p (m t) -> p m t", t=PACK)[:, :, 2 * u : 2 * u + 2],
+            )
+
+        a_bank = [ps.tile([P, J], F32, name=f"a_bank{t}") for t in range(PACK)]
+        b_bank = [ps.tile([P, J], F32, name=f"b_bank{t}") for t in range(PACK)]
+
+        def first_stage(bank, codes, plane, fmt, t, x_codes, x_scales):
+            nc.tensor.matmul_mx(
+                bank[t][:], lhsT=codes[t // 2][:, t % 2, :].bitcast(fmt), lhsT_scale=plane[:, t, :],
+                rhs=x_codes[:].bitcast(E4M3X4), rhs_scale=x_scales[:], start=True, stop=True,
+            )
+
+        def mm_a(t):
+            first_stage(a_bank, w_dealt, w_dealt_plane, E2M1X4, t, x1_codes, x1_plane)
+
+        def mm_b(t):
+            first_stage(b_bank, w2_dealt, w2_dealt_plane, E5M2X4, t, x2_codes, x2_plane)
+
+        mm_a(0)
+        mm_a(1)
+        mm_b(0)
+        mm_b(1)
+        mm_a(2)
+        mm_b(2)
+        mm_a(3)
+        mm_b(3)
+
+        a_rows = [sbuf(f"a_rows{t}", [P, J], F32) for t in range(PACK)]
+        b_rows = [sbuf(f"b_rows{t}", [P, J], F32) for t in range(PACK)]
+        diff = [sbuf(f"diff{t}", [P, 1], F32) for t in range(PACK)]
+        dl = [sbuf(f"dl{t}", [P, 1], F32) for t in range(PACK)]
+        a_picked = sbuf("a_picked", [P, PACK, O], F32)
+        b_picked = sbuf("b_picked", [P, PACK, O], F32)
+        for t in range(PACK):
+            if t < 2:
+                nc.scalar.copy(a_rows[t][:], a_bank[t][:])
+            else:
+                nc.vector.tensor_copy(a_rows[t][:], a_bank[t][:])
+            nc.vector.tensor_scalar(diff[t][:], b_bank[t][:, 0:1], b_bank[t][:, 128:129], None, ALU.subtract)
+            nc.vector.tensor_copy(b_rows[t][:], b_bank[t][:])
+            nc.vector.scalar_tensor_tensor(dl[t][:], diff[t][:], -1.0, diff[t][:], ALU.mult, ALU.max)
+        for t in range(PACK):
+            nc.scalar.activation(b_picked[:, t, :], b_rows[t][:].indirect(list4[:]), COPY, scale=a_rows[t][:, 0:1])
+            nc.scalar.activation(a_picked[:, t, :], a_rows[t][:].indirect(list3[:]), COPY, scale=dl[t][:])
+
+        hid = sbuf("hid", [P, O, PACK], BF16)
+        nc.vector.tensor_tensor(
+            hid[:].rearrange("p (c i) t -> p c t i", i=4),
+            a_picked[:].rearrange("p t (c i) -> p c t i", i=4),
+            b_picked[:].rearrange("p t (c i) -> p c t i", i=4),
+            ALU.max,
+        )
+        hid_codes = sbuf("hid_codes", [P, O], U32)
+        hid_plane = sbuf("hid_plane", [P, O], U8)
+        nc.vector.quantize_mx(hid_codes[:].bitcast(E4M3X4), hid_plane[:], hid[:].rearrange("p o t -> p (o t)"))
+
+        p_rows = []
+        for h in range(2):
+            cols = slice(P * h, P * (h + 1))
+            p_bank = ps.tile([P, O], F32, name=f"a_bank{h}")
+            nc.tensor.matmul_mx(
+                p_bank[:], lhsT=wb_codes[:, cols].bitcast(E5M2X4), lhsT_scale=wb_plane[:, cols],
+                rhs=hid_codes[:].bitcast(E4M3X4), rhs_scale=hid_plane[:], start=True, stop=True,
+            )
+            p_rows.append(sbuf(f"p_rows{h}", [P, O], F32))
+            if h == 0:
+                nc.vector.tensor_copy(p_rows[h][:], p_bank[:])
+            else:
+                nc.scalar.copy(p_rows[h][:], p_bank[:])
+        for h in range(2):
+            nc.vector.tensor_copy(pages["pa", h][:].indirect(list5[:]), p_rows[h][:])
+            nc.scalar.activation(pages["pb", h][:].indirect(list6[:]), p_rows[h][:], COPY)
+        for h in range(2):
+            for c in range(2):
+                cols = slice(E // 2 * c, E // 2 * (c + 1))
+                y = sbuf(f"y{h}{c}", [P, E // 2], F32)
+                nc.vector.tensor_tensor(y[:], pages["pa", h][:, cols], pages["pb", h][:, cols], ALU.add)
+                nc.sync.dma_start(out[P * h : P * (h + 1), cols], y[:])

@@ -45,106 +45,92 @@ def tile_list_contrast_ahead_one_pagetwice_kernel(
             nc.vector.memset(plane[:].bitcast(I32), 0)
             return plane
 
-        def stage_rows(queue, stage, scales, half):
-            rows = scales[0, 8 * half : 8 * half + 8, :].bitcast(I32)
-            queue.dma_start(stage[64 * half : 64 * half + 4, :, :], rows.rearrange("(q r) n -> r q n", q=2))
-
-        def spread_rows(plane, stage):
-            for q in range(QUADS):
-                src = 64 * (q // 2)
-                nc.vector.tensor_copy(plane[QUAD * q : QUAD * q + 4, :].bitcast(I32), stage[src : src + 4, q % 2, :])
-
-        def load_plane(plane, scales):
-            for r in range(4):
-                nc.sync.dma_start(plane[r:P:QUAD, :].bitcast(I32), scales[0, r:16:4, :].bitcast(I32))
+        def load_plane(plane, scales, queues):
+            for r, queue in enumerate(queues):
+                queue.dma_start(plane[r:P:QUAD, :].bitcast(I32), scales[0, r:16:4, :].bitcast(I32))
 
         def load_words(queue, tile, words):
             queue.dma_start(tile[:].bitcast(I32), words.bitcast(I32))
 
+        x_plane = sbuf("x_plane", [P, T], U8)
+        nc.vector.memset(x_plane[:, 0:1280].bitcast(I32), 0)
+        nc.gpsimd.memset(x_plane[:, 1280:T].bitcast(I32), 0)
+        w_stage = sbuf("w_stage", [P, QUADS, R // 4], I32)
+        nc.vector.memset(w_stage[64:96, 0:2, :], 0)
         w2_plane = zeroed_plane("w2_plane", R)
-        x_plane = zeroed_plane("x_plane", T)
         w_plane = zeroed_plane("w_plane", R)
         wb_plane = zeroed_plane("wb_plane", N)
 
-        x_stage = sbuf("x_stage", [P, 2, T // 4], I32)
-        w_stage = sbuf("w_stage", [P, 2, R // 4], I32)
+        w2_stage = sbuf("w2_stage", [4, QUADS, R // 4], I32)
         x_table = sbuf("x_table", [P, T], U32)
         w_raw = sbuf("w_raw", [P, R], U16)
         w2_raw = sbuf("w2_raw", [P, R], U32)
         wb_codes = sbuf("wb_codes", [P, N], U32)
 
-        stage_rows(nc.sync, x_stage, xt_scales, 0)
-        stage_rows(nc.scalar, x_stage, xt_scales, 1)
-        list1 = load_list("list1", offs)
-        stage_rows(nc.scalar, w_stage, w_scales, 0)
         list2 = load_list("list2", offs2)
-        stage_rows(nc.scalar, w_stage, w_scales, 1)
-        list4 = load_list("list4", offs4)
+        nc.scalar.dma_start(w2_stage[:], w2_scales[0].bitcast(I32).rearrange("(q r) n -> r q n", q=QUADS))
+        load_plane(x_plane, xt_scales, [nc.scalar, nc.sync, nc.scalar, nc.sync])
+        nc.sync.dma_start(w_stage[64:68], w_scales[0].bitcast(I32).rearrange("(q r) n -> r q n", q=QUADS))
         load_words(nc.scalar, x_table, xt_words[0].rearrange("p n t -> p (n t)"))
-        load_words(nc.scalar, w_raw, w_words[0])
+        list1 = load_list("list1", offs)
         load_words(nc.scalar, w2_raw, w2_words[0].rearrange("p n t -> p (n t)"))
-        load_plane(w2_plane, w2_scales)
+        load_words(nc.scalar, w_raw, w_words[0])
         list3 = load_list("list3", offs3)
+        list4 = load_list("list4", offs4)
         load_words(nc.sync, wb_codes, wb_words[0].rearrange("p n t -> p (n t)"))
-        load_plane(wb_plane, wb_scales)
+        load_plane(wb_plane, wb_scales, [nc.sync] * 4)
         list5 = load_list("list5", offs5)
         list6 = load_list("list6", offs6)
 
-        pages = {}
-        for h in range(2):
-            for name in ("pa", "pb"):
-                pages[name, h] = sbuf(f"{name}{h}", [P, E], F32)
-                nc.vector.memset(pages[name, h][:], 0.0)
-
-        spread_rows(x_plane, x_stage)
-        spread_rows(w_plane, w_stage)
+        for q in range(QUADS):
+            nc.vector.tensor_copy(w2_plane[QUAD * q : QUAD * q + 4, :].bitcast(I32), w2_stage[:, q, :])
+        for q in range(QUADS):
+            rows = QUAD if q < 2 else 4
+            nc.vector.tensor_copy(w_plane[QUAD * q : QUAD * q + rows, :].bitcast(I32), w_stage[64 : 64 + rows, q, :])
         w_dealt_plane = sbuf("w_dealt_plane", [P, PACK, P], U8)
         w2_dealt_plane = sbuf("w2_dealt_plane", [P, PACK, P], U8)
-        nc.vector.tensor_copy(w_dealt_plane[:], w_plane[:].rearrange("p (m t) -> p t m", t=PACK))
-        nc.gpsimd.tensor_copy(w2_dealt_plane[:], w2_plane[:].rearrange("p (m t) -> p t m", t=PACK))
+        nc.vector.tensor_copy(w2_dealt_plane[:], w2_plane[:].rearrange("p (m t) -> p t m", t=PACK))
 
         x1_codes = sbuf("x1_codes", [P, J], U32)
         x2_codes = sbuf("x2_codes", [P, J], U32)
         x1_plane = sbuf("x1_plane", [P, J], U8)
         x2_plane = sbuf("x2_plane", [P, J], U8)
-        nc.vector.tensor_copy(x1_plane[:], x_plane[:].indirect(list1[:]))
         nc.vector.tensor_copy(x2_plane[:], x_plane[:].indirect(list2[:]))
-        nc.vector.tensor_copy(x1_codes[:], x_table[:].indirect(list1[:]))
+        nc.vector.tensor_copy(w_dealt_plane[:], w_plane[:].rearrange("p (m t) -> p t m", t=PACK))
+        nc.vector.tensor_copy(x1_plane[:], x_plane[:].indirect(list1[:]))
         nc.vector.tensor_copy(x2_codes[:], x_table[:].indirect(list2[:]))
+        nc.vector.tensor_copy(x1_codes[:], x_table[:].indirect(list1[:]))
 
-        w_dealt = [sbuf(f"w_dealt{u}", [P, 2, P], U16) for u in range(2)]
-        w2_dealt = [sbuf(f"w2_dealt{u}", [P, 2, P], U32) for u in range(2)]
-        for u in range(2):
-            nc.scalar.copy(w_dealt[u][:], w_raw[:].rearrange("p (m t) -> p t m", t=PACK)[:, 2 * u : 2 * u + 2, :])
-        for u in range(2):
+        def deal_w2(tile, u):
             nc.scalar.copy(
-                w2_dealt[u][:].rearrange("p t m -> p m t"),
+                tile[:].rearrange("p t m -> p m t"),
                 w2_raw[:].rearrange("p (m t) -> p m t", t=PACK)[:, :, 2 * u : 2 * u + 2],
             )
+            return tile
+
+        w2_dealt = [deal_w2(sbuf("w2_dealt0", [P, 2, P], U32), 0)]
+        w_dealt = [sbuf(f"w_dealt{t}", [P, P], U16) for t in range(PACK)]
+        for t in range(PACK):
+            nc.scalar.copy(w_dealt[t][:], w_raw[:, t:R:PACK])
+        w2_dealt.append(deal_w2(sbuf("w_raw", [P, 2, P], U32), 1))
 
         a_bank = [ps.tile([P, J], F32, name=f"a_bank{t}") for t in range(PACK)]
         b_bank = [ps.tile([P, J], F32, name=f"b_bank{t}") for t in range(PACK)]
 
-        def first_stage(bank, codes, plane, fmt, t, x_codes, x_scales):
+        for t in range(PACK):
             nc.tensor.matmul_mx(
-                bank[t][:], lhsT=codes[t // 2][:, t % 2, :].bitcast(fmt), lhsT_scale=plane[:, t, :],
-                rhs=x_codes[:].bitcast(E4M3X4), rhs_scale=x_scales[:], start=True, stop=True,
+                b_bank[t][:], lhsT=w2_dealt[t // 2][:, t % 2, :].bitcast(E5M2X4), lhsT_scale=w2_dealt_plane[:, t, :],
+                rhs=x2_codes[:].bitcast(E4M3X4), rhs_scale=x2_plane[:], start=True, stop=True,
+            )
+            nc.tensor.matmul_mx(
+                a_bank[t][:], lhsT=w_dealt[t][:].bitcast(E2M1X4), lhsT_scale=w_dealt_plane[:, t, :],
+                rhs=x1_codes[:].bitcast(E4M3X4), rhs_scale=x1_plane[:], start=True, stop=True,
             )
 
-        def mm_a(t):
-            first_stage(a_bank, w_dealt, w_dealt_plane, E2M1X4, t, x1_codes, x1_plane)
-
-        def mm_b(t):
-            first_stage(b_bank, w2_dealt, w2_dealt_plane, E5M2X4, t, x2_codes, x2_plane)
-
-        mm_a(0)
-        mm_a(1)
-        mm_b(0)
-        mm_b(1)
-        mm_a(2)
-        mm_b(2)
-        mm_a(3)
-        mm_b(3)
+        pages = {}
+        for page, tag in zip([("pa", 0), ("pb", 0), ("pa", 1), ("pb", 1)], ["w_dealt0", "w2_dealt0", "w_dealt1", "w2_raw"]):
+            pages[page] = sbuf(tag, [P, E], F32)
+            nc.gpsimd.memset(pages[page][:], 0.0)
 
         a_rows = [sbuf(f"a_rows{t}", [P, J], F32) for t in range(PACK)]
         b_rows = [sbuf(f"b_rows{t}", [P, J], F32) for t in range(PACK)]
@@ -153,32 +139,41 @@ def tile_list_contrast_ahead_one_pagetwice_kernel(
         a_picked = sbuf("a_picked", [P, PACK, O], F32)
         b_picked = sbuf("b_picked", [P, PACK, O], F32)
         for t in range(PACK):
-            if t < 2:
-                nc.scalar.copy(a_rows[t][:], a_bank[t][:])
-            else:
-                nc.vector.tensor_copy(a_rows[t][:], a_bank[t][:])
             nc.vector.tensor_scalar(diff[t][:], b_bank[t][:, 0:1], b_bank[t][:, 128:129], None, ALU.subtract)
             nc.vector.tensor_copy(b_rows[t][:], b_bank[t][:])
             nc.vector.scalar_tensor_tensor(dl[t][:], diff[t][:], -1.0, diff[t][:], ALU.mult, ALU.max)
+            nc.vector.tensor_copy(a_rows[t][:], a_bank[t][:])
         for t in range(PACK):
-            nc.scalar.activation(b_picked[:, t, :], b_rows[t][:].indirect(list4[:]), COPY, scale=a_rows[t][:, 0:1])
             nc.scalar.activation(a_picked[:, t, :], a_rows[t][:].indirect(list3[:]), COPY, scale=dl[t][:])
+            if t < PACK - 1:
+                nc.scalar.activation(b_picked[:, t, :], b_rows[t][:].indirect(list4[:]), COPY, scale=a_rows[t][:, 0:1])
+            else:
+                for g in range(2):
+                    nc.scalar.activation(
+                        b_picked[:, t, 64 * g : 64 * g + 64], b_rows[t][:].indirect(list4[:, 4 * g : 4 * g + 4]),
+                        COPY, scale=a_rows[t][:, 0:1],
+                    )
 
         hid = sbuf("hid", [P, O, PACK], BF16)
-        nc.vector.tensor_tensor(
-            hid[:].rearrange("p (c i) t -> p c t i", i=4),
-            a_picked[:].rearrange("p t (c i) -> p c t i", i=4),
-            b_picked[:].rearrange("p t (c i) -> p c t i", i=4),
-            ALU.max,
-        )
         hid_codes = sbuf("hid_codes", [P, O], U32)
         hid_plane = sbuf("hid_plane", [P, O], U8)
-        nc.vector.quantize_mx(hid_codes[:].bitcast(E4M3X4), hid_plane[:], hid[:].rearrange("p o t -> p (o t)"))
+        for g in range(2):
+            places = slice(64 * g, 64 * g + 64)
+            nc.vector.tensor_tensor(
+                hid[:, places, :].rearrange("p (c i) t -> p c t i", i=4),
+                a_picked[:, :, places].rearrange("p t (c i) -> p c t i", i=4),
+                b_picked[:, :, places].rearrange("p t (c i) -> p c t i", i=4),
+                ALU.max,
+            )
+            nc.vector.quantize_mx(
+                hid_codes[:, places].bitcast(E4M3X4), hid_plane[:, places],
+                hid[:, places, :].rearrange("p o t -> p (o t)"),
+            )
 
         p_rows = []
         for h in range(2):
             cols = slice(P * h, P * (h + 1))
-            p_bank = ps.tile([P, O], F32, name=f"a_bank{h}")
+            p_bank = ps.tile([P, O], F32, name=f"b_bank{h}")
             nc.tensor.matmul_mx(
                 p_bank[:], lhsT=wb_codes[:, cols].bitcast(E5M2X4), lhsT_scale=wb_plane[:, cols],
                 rhs=hid_codes[:].bitcast(E4M3X4), rhs_scale=hid_plane[:], start=True, stop=True,

@@ -55,8 +55,7 @@ def tile_list_contrast_ahead_one_pagetwice_kernel(
         x_plane = sbuf("x_plane", [P, T], U8)
         nc.vector.memset(x_plane[:, 0:1280].bitcast(I32), 0)
         nc.gpsimd.memset(x_plane[:, 1280:T].bitcast(I32), 0)
-        w_stage = sbuf("w_stage", [P, QUADS, R // 4], I32)
-        nc.vector.memset(w_stage[64:96, 0:2, :], 0)
+        w_stage = sbuf("w_stage", [4, QUADS, R // 4], I32)
         w2_plane = zeroed_plane("w2_plane", R)
         w_plane = zeroed_plane("w_plane", R)
         wb_plane = zeroed_plane("wb_plane", N)
@@ -69,8 +68,8 @@ def tile_list_contrast_ahead_one_pagetwice_kernel(
 
         list2 = load_list("list2", offs2)
         nc.scalar.dma_start(w2_stage[:], w2_scales[0].bitcast(I32).rearrange("(q r) n -> r q n", q=QUADS))
+        nc.sync.dma_start(w_stage[:], w_scales[0].bitcast(I32).rearrange("(q r) n -> r q n", q=QUADS))
         load_plane(x_plane, xt_scales, [nc.scalar, nc.sync, nc.scalar, nc.sync])
-        nc.sync.dma_start(w_stage[64:68], w_scales[0].bitcast(I32).rearrange("(q r) n -> r q n", q=QUADS))
         load_words(nc.scalar, x_table, xt_words[0].rearrange("p n t -> p (n t)"))
         list1 = load_list("list1", offs)
         load_words(nc.scalar, w2_raw, w2_words[0].rearrange("p n t -> p (n t)"))
@@ -85,8 +84,7 @@ def tile_list_contrast_ahead_one_pagetwice_kernel(
         for q in range(QUADS):
             nc.vector.tensor_copy(w2_plane[QUAD * q : QUAD * q + 4, :].bitcast(I32), w2_stage[:, q, :])
         for q in range(QUADS):
-            rows = QUAD if q < 2 else 4
-            nc.vector.tensor_copy(w_plane[QUAD * q : QUAD * q + rows, :].bitcast(I32), w_stage[64 : 64 + rows, q, :])
+            nc.vector.tensor_copy(w_plane[QUAD * q : QUAD * q + 4, :].bitcast(I32), w_stage[:, q, :])
         w_dealt_plane = sbuf("w_dealt_plane", [P, PACK, P], U8)
         w2_dealt_plane = sbuf("w2_dealt_plane", [P, PACK, P], U8)
         nc.vector.tensor_copy(w2_dealt_plane[:], w2_plane[:].rearrange("p (m t) -> p t m", t=PACK))
@@ -142,7 +140,10 @@ def tile_list_contrast_ahead_one_pagetwice_kernel(
             nc.vector.tensor_scalar(diff[t][:], b_bank[t][:, 0:1], b_bank[t][:, 128:129], None, ALU.subtract)
             nc.vector.tensor_copy(b_rows[t][:], b_bank[t][:])
             nc.vector.scalar_tensor_tensor(dl[t][:], diff[t][:], -1.0, diff[t][:], ALU.mult, ALU.max)
-            nc.vector.tensor_copy(a_rows[t][:], a_bank[t][:])
+            if t == 0:
+                nc.scalar.copy(a_rows[t][:], a_bank[t][:])
+            else:
+                nc.vector.tensor_copy(a_rows[t][:], a_bank[t][:])
         for t in range(PACK):
             nc.scalar.activation(a_picked[:, t, :], a_rows[t][:].indirect(list3[:]), COPY, scale=dl[t][:])
             if t < PACK - 1:

from contextlib import ExitStack

import concourse.mybir as mybir

K, T, J, R, O, N, E = 512, 2048, 256, 512, 128, 256, 512
FLOPS = 2 * K * R * J * 2 + 2 * R * N * O

F32 = mybir.dt.float32
BF16 = mybir.dt.bfloat16
I32 = mybir.dt.int32
U32 = mybir.dt.uint32
U16 = mybir.dt.uint16
U8 = mybir.dt.uint8
E4M3X4 = mybir.dt.float8_e4m3fn_x4
E5M2X4 = mybir.dt.float8_e5m2_x4
E2M1X4 = mybir.dt.float4_e2m1fn_x4
ALU = mybir.AluOpType
COPY = mybir.ActivationFunctionType.Copy

P = 128
PACK = 4
QUADS = 4
QUAD = 32


def tile_list_contrast_ahead_one_pagetwice_kernel(
    tc, xt_words, xt_scales, w_words, w_scales, w2_words, w2_scales, wb_words, wb_scales,
    offs, offs2, offs3, offs4, offs5, offs6, out,
):
    nc = tc.nc
    with ExitStack() as ctx:
        sb = ctx.enter_context(tc.tile_pool(name="sb", bufs=1))
        ps = ctx.enter_context(tc.psum_pool(name="ps", bufs=1))

        def sbuf(name, shape, dtype):
            return sb.tile(shape, dtype, name=name, align_bytes=64)

        def load_list(name, src):
            tile = sbuf(name, list(src.shape), U16)
            nc.sync.dma_start(tile[:], src)
            return tile

        def zeroed_plane(name, columns):
            plane = sbuf(name, [P, columns], U8)
            nc.vector.memset(plane[:].bitcast(I32), 0)
            return plane

        def load_plane(plane, scales, queues):
            for r, queue in enumerate(queues):
                queue.dma_start(plane[r:P:QUAD, :].bitcast(I32), scales[0, r:16:4, :].bitcast(I32))

        def load_words(queue, tile, words):
            queue.dma_start(tile[:].bitcast(I32), words.bitcast(I32))

        x_plane = sbuf("x_plane", [P, T], U8)
        nc.vector.memset(x_plane[:, 0:1280].bitcast(I32), 0)
        nc.gpsimd.memset(x_plane[:, 1280:T].bitcast(I32), 0)
        w_stage = sbuf("w_stage", [4, QUADS, R // 4], I32)
        w2_plane = zeroed_plane("w2_plane", R)
        w_plane = zeroed_plane("w_plane", R)
        wb_plane = zeroed_plane("wb_plane", N)

        w2_stage = sbuf("w2_stage", [4, QUADS, R // 4], I32)
        x_table = sbuf("x_table", [P, T], U32)
        w_raw = sbuf("w_raw", [P, R], U16)
        w2_raw = sbuf("w2_raw", [P, R], U32)
        wb_codes = sbuf("wb_codes", [P, N], U32)

        list2 = load_list("list2", offs2)
        nc.scalar.dma_start(w2_stage[:], w2_scales[0].bitcast(I32).rearrange("(q r) n -> r q n", q=QUADS))
        nc.sync.dma_start(w_stage[:], w_scales[0].bitcast(I32).rearrange("(q r) n -> r q n", q=QUADS))
        load_plane(x_plane, xt_scales, [nc.scalar, nc.sync, nc.scalar, nc.sync])
        load_words(nc.scalar, x_table, xt_words[0].rearrange("p n t -> p (n t)"))
        list1 = load_list("list1", offs)
        load_words(nc.scalar, w2_raw, w2_words[0].rearrange("p n t -> p (n t)"))
        load_words(nc.scalar, w_raw, w_words[0])
        list3 = load_list("list3", offs3)
        list4 = load_list("list4", offs4)
        load_words(nc.sync, wb_codes, wb_words[0].rearrange("p n t -> p (n t)"))
        load_plane(wb_plane, wb_scales, [nc.sync] * 4)
        list5 = load_list("list5", offs5)
        list6 = load_list("list6", offs6)

        for q in range(QUADS):
            nc.vector.tensor_copy(w2_plane[QUAD * q : QUAD * q + 4, :].bitcast(I32), w2_stage[:, q, :])
        for q in range(QUADS):
            nc.vector.tensor_copy(w_plane[QUAD * q : QUAD * q + 4, :].bitcast(I32), w_stage[:, q, :])
        w_dealt_plane = sbuf("w_dealt_plane", [P, PACK, P], U8)
        w2_dealt_plane = sbuf("w2_dealt_plane", [P, PACK, P], U8)
        nc.vector.tensor_copy(w2_dealt_plane[:], w2_plane[:].rearrange("p (m t) -> p t m", t=PACK))

        x1_codes = sbuf("x1_codes", [P, J], U32)
        x2_codes = sbuf("x2_codes", [P, J], U32)
        x1_plane = sbuf("x1_plane", [P, J], U8)
        x2_plane = sbuf("x2_plane", [P, J], U8)
        nc.vector.tensor_copy(x2_plane[:], x_plane[:].indirect(list2[:]))
        nc.vector.tensor_copy(w_dealt_plane[:], w_plane[:].rearrange("p (m t) -> p t m", t=PACK))
        nc.vector.tensor_copy(x1_plane[:], x_plane[:].indirect(list1[:]))
        nc.vector.tensor_copy(x2_codes[:], x_table[:].indirect(list2[:]))
        nc.vector.tensor_copy(x1_codes[:], x_table[:].indirect(list1[:]))

        def deal_w2(tile, u):
            nc.scalar.copy(
                tile[:].rearrange("p t m -> p m t"),
                w2_raw[:].rearrange("p (m t) -> p m t", t=PACK)[:, :, 2 * u : 2 * u + 2],
            )
            return tile

        w2_dealt = [deal_w2(sbuf("w2_dealt0", [P, 2, P], U32), 0)]
        w_dealt = [sbuf(f"w_dealt{t}", [P, P], U16) for t in range(PACK)]
        for t in range(PACK):
            nc.scalar.copy(w_dealt[t][:], w_raw[:, t:R:PACK])
        w2_dealt.append(deal_w2(sbuf("w_raw", [P, 2, P], U32), 1))

        a_bank = [ps.tile([P, J], F32, name=f"a_bank{t}") for t in range(PACK)]
        b_bank = [ps.tile([P, J], F32, name=f"b_bank{t}") for t in range(PACK)]

        for t in range(PACK):
            nc.tensor.matmul_mx(
                b_bank[t][:], lhsT=w2_dealt[t // 2][:, t % 2, :].bitcast(E5M2X4), lhsT_scale=w2_dealt_plane[:, t, :],
                rhs=x2_codes[:].bitcast(E4M3X4), rhs_scale=x2_plane[:], start=True, stop=True,
            )
            nc.tensor.matmul_mx(
                a_bank[t][:], lhsT=w_dealt[t][:].bitcast(E2M1X4), lhsT_scale=w_dealt_plane[:, t, :],
                rhs=x1_codes[:].bitcast(E4M3X4), rhs_scale=x1_plane[:], start=True, stop=True,
            )

        pages = {}
        for page, tag in zip([("pa", 0), ("pb", 0), ("pa", 1), ("pb", 1)], ["w_dealt0", "w2_dealt0", "w_dealt1", "w2_raw"]):
            pages[page] = sbuf(tag, [P, E], F32)
            nc.gpsimd.memset(pages[page][:], 0.0)

        a_rows = [sbuf(f"a_rows{t}", [P, J], F32) for t in range(PACK)]
        b_rows = [sbuf(f"b_rows{t}", [P, J], F32) for t in range(PACK)]
        diff = [sbuf(f"diff{t}", [P, 1], F32) for t in range(PACK)]
        dl = [sbuf(f"dl{t}", [P, 1], F32) for t in range(PACK)]
        a_picked = sbuf("a_picked", [P, PACK, O], F32)
        b_picked = sbuf("b_picked", [P, PACK, O], F32)
        for t in range(PACK):
            nc.vector.tensor_scalar(diff[t][:], b_bank[t][:, 0:1], b_bank[t][:, 128:129], None, ALU.subtract)
            nc.vector.tensor_copy(b_rows[t][:], b_bank[t][:])
            nc.vector.scalar_tensor_tensor(dl[t][:], diff[t][:], -1.0, diff[t][:], ALU.mult, ALU.max)
            if t == 0:
                nc.scalar.copy(a_rows[t][:], a_bank[t][:])
            else:
                nc.vector.tensor_copy(a_rows[t][:], a_bank[t][:])
        for t in range(PACK):
            nc.scalar.activation(a_picked[:, t, :], a_rows[t][:].indirect(list3[:]), COPY, scale=dl[t][:])
            if t < PACK - 1:
                nc.scalar.activation(b_picked[:, t, :], b_rows[t][:].indirect(list4[:]), COPY, scale=a_rows[t][:, 0:1])
            else:
                for g in range(2):
                    nc.scalar.activation(
                        b_picked[:, t, 64 * g : 64 * g + 64], b_rows[t][:].indirect(list4[:, 4 * g : 4 * g + 4]),
                        COPY, scale=a_rows[t][:, 0:1],
                    )

        hid = sbuf("hid", [P, O, PACK], BF16)
        hid_codes = sbuf("hid_codes", [P, O], U32)
        hid_plane = sbuf("hid_plane", [P, O], U8)
        for g in range(2):
            places = slice(64 * g, 64 * g + 64)
            nc.vector.tensor_tensor(
                hid[:, places, :].rearrange("p (c i) t -> p c t i", i=4),
                a_picked[:, :, places].rearrange("p t (c i) -> p c t i", i=4),
                b_picked[:, :, places].rearrange("p t (c i) -> p c t i", i=4),
                ALU.max,
            )
            nc.vector.quantize_mx(
                hid_codes[:, places].bitcast(E4M3X4), hid_plane[:, places],
                hid[:, places, :].rearrange("p o t -> p (o t)"),
            )

        p_rows = []
        for h in range(2):
            cols = slice(P * h, P * (h + 1))
            p_bank = ps.tile([P, O], F32, name=f"b_bank{h}")
            nc.tensor.matmul_mx(
                p_bank[:], lhsT=wb_codes[:, cols].bitcast(E5M2X4), lhsT_scale=wb_plane[:, cols],
                rhs=hid_codes[:].bitcast(E4M3X4), rhs_scale=hid_plane[:], start=True, stop=True,
            )
            p_rows.append(sbuf(f"p_rows{h}", [P, O], F32))
            if h == 0:
                nc.vector.tensor_copy(p_rows[h][:], p_bank[:])
            else:
                nc.scalar.copy(p_rows[h][:], p_bank[:])
        for h in range(2):
            nc.vector.tensor_copy(pages["pa", h][:].indirect(list5[:]), p_rows[h][:])
            nc.scalar.activation(pages["pb", h][:].indirect(list6[:]), p_rows[h][:], COPY)
        for h in range(2):
            for c in range(2):
                cols = slice(E // 2 * c, E // 2 * (c + 1))
                y = sbuf(f"y{h}{c}", [P, E // 2], F32)
                nc.vector.tensor_tensor(y[:], pages["pa", h][:, cols], pages["pb", h][:, cols], ALU.add)
                nc.sync.dma_start(out[P * h : P * (h + 1), cols], y[:])
